import numpy as np
import ml_dtypes


def mxq(x, axis, fmt="e4m3"):
    dtype, down = {"e4m3": (ml_dtypes.float8_e4m3fn, 7), "e5m2": (ml_dtypes.float8_e5m2, 14)}[fmt]
    v = np.moveaxis(np.asarray(x, np.float32).astype(ml_dtypes.bfloat16).astype(np.float64), axis, -1)
    blocks = v.reshape(v.shape[:-1] + (-1, 32))
    amax = np.abs(blocks).max(-1, keepdims=True)
    byte = np.maximum(np.where(amax > 0, np.frexp(amax)[1] - 1 + 127, 0) - down, 1)
    scale = np.exp2(byte - 127.0)
    codes = (blocks / scale).astype(np.float32).astype(dtype).astype(np.float64)
    return np.moveaxis((codes * scale).reshape(v.shape), -1, axis)


WIDE = False


def mx_kscale(k):
    if not WIDE:
        return np.ones(k)
    levels = np.array([10, -10, 5, -5, 0])
    if k % 512:
        return np.exp2(np.random.permutation(np.resize(levels, k // 32))).repeat(32)
    a = np.empty((k // 512, 16))
    for p in range(k // 512):
        a[p, :8] = np.random.permutation(np.resize(levels, 8))
        for g in range(8):
            far = levels[np.abs(levels - a[p, g]) >= 10]
            a[p, g + 8] = far[np.random.randint(len(far))]
    return np.exp2(a.ravel()).repeat(32)


def f64(x):
    return np.asarray(x).astype(np.float64)


def striped(idx):
    return np.tile(idx.reshape(-1, 16).T, (8, 1)).astype(np.uint16)


def unstriped(offs):
    return offs[:16].T.reshape(-1).astype(np.int64)


E2M1 = np.array([0.0, 0.5, 1.0, 1.5, 2.0, 3.0, 4.0, 6.0, -0.0, -0.5, -1.0, -1.5, -2.0, -3.0, -4.0, -6.0])


def pack_weight(w, fmt):
    k, n = w.shape
    w = f64(np.asarray(w, np.float32).astype(ml_dtypes.bfloat16)).reshape(k // 32, 32, n)
    amax = np.abs(w).max(1)
    if fmt == "e4m3":
        byte = np.frexp(amax)[1] - 1 + 127 - 7
    else:
        mant, ex = np.frexp(amax / 6.0)
        byte = np.where(mant > 0.5, ex, ex - 1) + 127
    byte = np.clip(np.where(amax > 0, byte, 1), 1, 254)
    scaled = (w * np.exp2(127.0 - byte)[:, None, :]).reshape(k, n).astype(np.float32)
    by_word = np.ascontiguousarray(scaled.reshape(k // 512, 128, 4, n).transpose(0, 1, 3, 2))
    if fmt == "e4m3":
        words = by_word.astype(ml_dtypes.float8_e4m3fn).view(np.uint8)
    else:
        c = by_word.astype(ml_dtypes.float4_e2m1fn).view(np.uint8) & 0xF
        words = (c[..., 0::2] | (c[..., 1::2] << 4)).reshape(k // 512, 128, 2 * n)
    return np.ascontiguousarray(words), np.ascontiguousarray(byte.astype(np.uint8).reshape(k // 512, 16, n))


def unpack_weight(words, scales, fmt):
    g, _, n = scales.shape
    words = np.ascontiguousarray(words).reshape(g, 128, n, -1)
    if fmt == "e4m3":
        vals = words.view(ml_dtypes.float8_e4m3fn).astype(np.float64)
    else:
        nib = np.empty((g, 128, n, 4), np.uint8)
        nib[..., 0::2] = words & 0xF
        nib[..., 1::2] = words >> 4
        vals = E2M1[nib]
    vals = vals * np.repeat(np.exp2(scales.astype(np.float64) - 127.0), 8, axis=1)[..., None]
    return vals.transpose(0, 1, 3, 2).reshape(g * 512, n)


def gelu(v):
    return 0.5 * v * (1.0 + np.tanh(np.sqrt(2.0 / np.pi) * (v + 0.044715 * v**3)))


def often(T, S):
    return np.random.permutation(T)[(T * np.random.uniform(0, 1, S) ** 4).astype(np.int64)]


K1, K2, H, N, T, S, P = 1024, 512, 1024, 384, 4096, 1024, 512


def setup_inputs():
    n = np.random.standard_normal
    s1 = mx_kscale(K1)[:, None]
    s2 = mx_kscale(K2)[:, None]
    u = mx_kscale(H)[:, None]
    d = {}
    d["tab_words"], d["tab_scales"] = pack_weight(n((K1, T)) * s1, "e4m3")
    d["tab2_words"], d["tab2_scales"] = pack_weight(n((K2, T)) * s2, "e4m3")
    d["tab3_words"], d["tab3_scales"] = pack_weight(n((K2, T)) * s2, "e4m3")
    d["offs"] = striped(np.random.permutation(T)[:S])
    d["offs2"] = striped(np.random.permutation(T)[:S])
    d["offs3"] = striped(np.random.permutation(T)[:S])
    d["pos1"] = striped(np.random.permutation(S)[:P])
    d["pos2"] = striped(often(S, P))
    d["pos3"] = striped(often(S, P))
    d["w1"] = (0.38 * n((K1, H)) / s1 / K1 ** 0.5).astype(np.float32)
    d["w2_words"], d["w2_scales"] = pack_weight(0.58 * n((K2, H)) / s2 / K2 ** 0.5, "e4m3")
    d["w3_words"], d["w3_scales"] = pack_weight(0.5 * n((K2, H)) / s2 / K2 ** 0.5, "e2m1")
    d["b1"] = np.random.uniform(-1.6, 0.1, H).astype(np.float32)
    d["zg"] = (np.exp(0.3 * n(H)) * u[:, 0]).astype(np.float32)
    d["w4"] = (1.2 * n((H, N)) / u / H ** 0.5).astype(np.float32)
    d["lobe"] = np.exp(0.4 * n(N)).astype(np.float32)
    return d


def reference(tab_words, tab_scales, tab2_words, tab2_scales, tab3_words, tab3_scales, offs, offs2, offs3,
              pos1, pos2, pos3, w1, w2_words, w2_scales, w3_words, w3_scales, b1, zg, w4, lobe):
    v = unpack_weight(tab_words, tab_scales, "e4m3")[:, unstriped(offs)]
    v2 = unpack_weight(tab2_words, tab2_scales, "e4m3")[:, unstriped(offs2)]
    v3 = unpack_weight(tab3_words, tab3_scales, "e4m3")[:, unstriped(offs3)]
    a = (mxq(f64(w1), 0, "e4m3").T @ v) + f64(b1)[:, None]
    b = unpack_weight(w2_words, w2_scales, "e4m3").T @ v2
    d = unpack_weight(w3_words, w3_scales, "e2m1").T @ v3
    wave = np.sin(a[:, unstriped(pos1)] + np.cos(b[:, unstriped(pos2)]))
    z = (wave - d[:, unstriped(pos3)]) * f64(zg)[:, None]
    y = mxq(f64(w4), 0, "e4m3").T @ mxq(z, 0, "e4m3")
    return y * f64(lobe)[:, None]

import math
from contextlib import ExitStack

import concourse.mybir as mybir
from concourse.masks import make_identity

K1, K2, H, N, T, S, J = 1024, 512, 1024, 384, 4096, 1024, 512
FLOPS = 2 * (K1 * H * S + 2 * K2 * H * S + H * N * J)

F32 = mybir.dt.float32
BF16 = mybir.dt.bfloat16
I32 = mybir.dt.int32
U32 = mybir.dt.uint32
U16 = mybir.dt.uint16
U8 = mybir.dt.uint8
FP8X4 = mybir.dt.float8_e4m3fn_x4
FP4X4 = mybir.dt.float4_e2m1fn_x4
ACT = mybir.ActivationFunctionType
ALU = mybir.AluOpType

P = 128
PACK = 4
K_PASS = P * PACK
BANK = 512
SLICES = H // P
GROUPS = 16
RUN = 8


def tile_list_camshaft_lobe_scores_kernel(
    tc, tab_words, tab_scales, tab2_words, tab2_scales, tab3_words, tab3_scales,
    offs, offs2, offs3, pos1, pos2, pos3, w1, w2_words, w2_scales, w3_words, w3_scales,
    b1, zg, w4, lobe, out,
):
    nc = tc.nc
    with ExitStack() as ctx:
        keep = ctx.enter_context(tc.tile_pool(name="keep", bufs=1))
        big = ctx.enter_context(tc.tile_pool(name="big", bufs=4))
        ring = ctx.enter_context(tc.tile_pool(name="ring", bufs=2))
        wins = ctx.enter_context(tc.tile_pool(name="wins", bufs=5))
        psum = ctx.enter_context(tc.psum_pool(name="psum", bufs=5))
        psum_out = ctx.enter_context(tc.psum_pool(name="psum_out", bufs=1))

        def load_list(name, src):
            t = keep.tile(list(src.shape), U16, name=name)
            nc.sync.dma_start(t[:], src)
            return t

        def zeroed_bytes(name, width, engine):
            t = keep.tile([P, width], U8, name=name, align_bytes=64)
            engine.memset(t[:].bitcast(I32), 0)
            return t

        def load_scale_rows(tile, rows, queue):
            for q in range(4):
                queue.dma_start(tile[:].bitcast(I32)[32 * q : 32 * q + 4, :], rows.bitcast(I32)[4 * q : 4 * q + 4, :])

        def load_table_words(words):
            t = big.tile([P, T], U32, name="table", tag="big", align_bytes=64)
            nc.sync.dma_start(t[:].bitcast(I32), words.rearrange("p n i -> p (n i)").bitcast(I32))
            return t

        def deal(name, src, dtype):
            t = keep.tile(list(src.shape), dtype, name=name, align_bytes=64)
            nc.vector.tensor_copy(
                t[:].bitcast(I32).rearrange("p (b t g q) -> p b t g q", b=2, t=PACK, g=GROUPS),
                src[:].bitcast(I32).rearrange("p (b g t q) -> p b t g q", b=2, t=PACK, g=GROUPS),
            )
            return t

        def gather(name, window, offsets, dtype, pieces=1):
            t = keep.tile([P, S], dtype, name=name, align_bytes=64)
            n, c = S // pieces, S // pieces // 16
            for i in range(pieces):
                nc.vector.tensor_copy(t[:, i * n : (i + 1) * n], window[:].indirect(offsets[:, i * c : (i + 1) * c]))
            return t

        sc1_win = big.tile([P, T], U8, name="sc1_win", tag="big", align_bytes=64)
        sc2_win = big.tile([P, T], U8, name="sc2_win", tag="big", align_bytes=64)
        sc3_win = big.tile([P, T], U8, name="sc3_win", tag="big", align_bytes=64)
        nc.vector.memset(sc2_win[:].bitcast(I32)[:, 0 : T // 8], 0)
        nc.gpsimd.memset(sc2_win[:].bitcast(I32)[:, T // 8 :], 0)
        w2s_raw = zeroed_bytes("w2s_raw", H, nc.vector)
        nc.vector.memset(sc1_win[:].bitcast(I32)[0:96, :], 0)
        nc.vector.memset(sc3_win[:].bitcast(I32), 0)
        w3s_raw = zeroed_bytes("w3s_raw", H, nc.gpsimd)
        rows = keep.tile([P, 2 * P], F32, name="rows")
        nc.gpsimd.memset(rows[:], 0.0)
        v1_scales = zeroed_bytes("v1_scales", 2 * S, nc.vector)

        def load_w1(b):
            t = big.tile([P, 2 * PACK * K_PASS], F32, name="w1_raw", tag="big", align_bytes=64)
            for a in range(2):
                nc.sync.dma_start(
                    t[:, a * PACK * K_PASS : (a + 1) * PACK * K_PASS].rearrange("p (j r) -> p j r", j=PACK),
                    w1[a * K_PASS : (a + 1) * K_PASS, b * K_PASS : (b + 1) * K_PASS].rearrange("(p j) r -> p j r", j=PACK),
                )
            return t

        idx1 = load_list("idx1", offs)
        for a in range(2):
            nc.sync.dma_start(sc1_win[:].bitcast(I32)[96 + a : P : 2, :], tab_scales[a].bitcast(I32))
        idx2 = load_list("idx2", offs2)
        load_scale_rows(sc2_win, tab2_scales[0], nc.scalar)
        tab2 = load_table_words(tab2_words[0])
        w2_raw = ring.tile([P, H], U32, name="w2_raw", tag="woven", align_bytes=64)
        nc.sync.dma_start(w2_raw[:].bitcast(I32), w2_words[0].rearrange("p n i -> p (n i)").bitcast(I32))
        load_scale_rows(w2s_raw, w2_scales[0], nc.scalar)
        idx3 = load_list("idx3", offs3)
        tab3 = load_table_words(tab3_words[0])
        load_scale_rows(sc3_win, tab3_scales[0], nc.scalar)
        w3_raw = keep.tile([P, 2 * H], U8, name="w3_raw")
        nc.sync.dma_start(w3_raw[:].bitcast(I32), w3_words[0].bitcast(I32))
        p2 = load_list("p2", pos2)
        tab1 = [load_table_words(tab_words[0])]
        p1 = load_list("p1", pos1)
        p3 = load_list("p3", pos3)
        w1_raw = [load_w1(0)]
        tab1.append(load_table_words(tab_words[1]))
        w1_raw.append(load_w1(1))
        for i, vec in enumerate((b1, zg)):
            nc.gpsimd.dma_start(
                rows[PACK * i : PACK * (i + 1), :].rearrange("t (g q) -> t g q", q=RUN),
                vec.rearrange("(g t q) -> t g q", t=PACK, q=RUN),
            )
        nc.gpsimd.dma_start(rows[8:11, 0:P], lobe.rearrange("(c n) -> c n", n=P))
        ident = keep.tile([P, P], F32, name="ident")
        make_identity(nc, ident[:])
        load_scale_rows(w3s_raw, w3_scales[0], nc.gpsimd)
        w4_raw = big.tile([P, SLICES * N], F32, name="w4_raw", tag="big", align_bytes=64)
        for s in range(SLICES):
            b, t = divmod(s, PACK)
            nc.sync.dma_start(
                w4_raw[:, s * N : (s + 1) * N],
                w4[b * K_PASS : (b + 1) * K_PASS, :].rearrange("(g t q) n -> t g q n", t=PACK, q=RUN)[t],
            )

        v1_scales_spread = gather("v1_scales_spread", sc1_win, idx1, U8)
        for q in range(4):
            nc.gpsimd.dma_start(
                v1_scales[:].bitcast(I32)[32 * q : 32 * q + 4, :],
                v1_scales_spread[:].bitcast(I32)[96 + 8 * q : 96 + 8 * q + 8, :],
            )
        v2_scales = gather("v2_scales", sc2_win, idx2, U8)
        v2 = gather("v2", tab2, idx2, U32, pieces=2)
        w2 = deal("w2", w2_raw, U32)
        w2s = deal("w2s", w2s_raw, U8)

        cols = keep.tile([P, 2, 12], F32, name="cols")
        a_bias = keep.tile([P, 2, PACK], F32, name="a_bias")
        neg_zg = keep.tile([P, 2, PACK], F32, name="neg_zg")
        neg2_zg = keep.tile([P, 2, PACK], F32, name="neg2_zg")

        def turn_vectors():
            turned = psum.tile([P, 2, P], F32, name="turned", tag="acc")
            for b in range(2):
                nc.tensor.transpose(turned[:, b, :], rows[:, b * P : (b + 1) * P], ident[:])
            nc.scalar.copy(cols[:], turned[:, :, 0:12])
            nc.gpsimd.tensor_scalar(a_bias[:], cols[:, :, 0:4], 0.5, 0.5 - math.pi / 4, ALU.mult, ALU.add)
            nc.gpsimd.tensor_scalar(neg_zg[:], cols[:, :, 4:8], -1.0, 0.0, ALU.mult, ALU.add)
            nc.gpsimd.tensor_scalar(neg2_zg[:], cols[:, :, 4:8], -2.0, 0.0, ALU.mult, ALU.add)

        def first_stage(window, passes, func, scale, bias):
            for h in range(S // BANK):
                cs = slice(h * BANK, (h + 1) * BANK)
                acc = psum.tile([P, BANK], F32, name="acc", tag="acc")
                for i, (w, ws, v, vs) in enumerate(passes):
                    nc.tensor.matmul_mx(
                        out=acc[:], lhsT=w, lhsT_scale=ws, rhs=v[:, cs].bitcast(FP8X4), rhs_scale=vs[:, cs],
                        start=(i == 0), stop=(i == len(passes) - 1),
                    )
                nc.scalar.activation(window[:, cs], acc[:], func, bias=bias, scale=scale)

        half_sin = []
        for s in range(SLICES):
            ms = slice(s * P, (s + 1) * P)
            b_win = wins.tile([P, S], F32, name="b_win", tag="win")
            first_stage(b_win, [(w2[:, ms].bitcast(FP8X4), w2s[:, ms], v2, v2_scales)], ACT.Sin, 0.5, 0.0)
            g = keep.tile([P, J], F32, name="half_sin%d" % s)
            nc.vector.tensor_copy(g[:], b_win[:].indirect(p2[:]))
            if s < PACK:
                nc.gpsimd.tensor_tensor(g[:], g[:], g[:], ALU.mult)
            half_sin.append(g[:])
            if s == 2:
                turn_vectors()

        v3_scales = gather("v3_scales", sc3_win, idx3, U8)
        v3 = gather("v3", tab3, idx3, U32)
        w3 = deal("w3", w3_raw, U8)
        w3s = deal("w3s", w3s_raw, U8)
        v1 = [gather("v1_0", tab1[0], idx1, U32)]

        d_wins = []

        def d_stage(s):
            b, t = divmod(s, PACK)
            d_win = keep.tile([P, S], F32, name="d_win%d" % s)
            first_stage(
                d_win,
                [(w3[:, 2 * s * P : 2 * (s + 1) * P].bitcast(FP4X4), w3s[:, s * P : (s + 1) * P], v3, v3_scales)],
                ACT.Identity, neg_zg[:, b, t : t + 1], cols[:, b, 4 + t : 5 + t],
            )
            d_wins.append(d_win)

        for s in range(SLICES):
            d_stage(s)

        w1_codes = keep.tile([P, 2, H], U32, name="w1_codes", align_bytes=64)
        w1_scales = keep.tile([P, 2, H], U8, name="w1_scales", align_bytes=64)

        def quantize_w1(b):
            for a in range(2):
                woven = ring.tile([P, PACK * K_PASS], BF16, name="woven", tag=("early", "woven")[b], align_bytes=64)
                src = w1_raw[b][:, a * PACK * K_PASS : (a + 1) * PACK * K_PASS].rearrange(
                    "p (j g t q) -> p t g q j", j=PACK, t=PACK, q=RUN)
                dst = woven[:].rearrange("p (t g q j) -> p t g q j", j=PACK, t=PACK, q=RUN)
                if b == 0:
                    for t in range(PACK):
                        nc.gpsimd.tensor_scalar(dst[:, t], src[:, t], 1.0, 0.0, ALU.mult, ALU.add)
                elif a == 0:
                    nc.scalar.copy(dst, src)
                else:
                    nc.vector.tensor_copy(dst, src)
                cs = slice(b * K_PASS, (b + 1) * K_PASS)
                nc.vector.quantize_mx(out=w1_codes[:, a, cs].bitcast(FP8X4), scales=w1_scales[:, a, cs], in_=woven[:])

        w4_codes = keep.tile([P, 2 * N], U32, name="w4_codes", align_bytes=64)
        w4_scales = keep.tile([P, 2 * N], U8, name="w4_scales", align_bytes=64)

        def quantize_w4():
            woven = keep.tile([P, 2 * N * PACK], BF16, name="w4_woven", align_bytes=64)
            for b in range(2):
                nc.scalar.copy(
                    woven[:, b * N * PACK : (b + 1) * N * PACK].rearrange("p (c i t) -> p c t i", t=PACK, i=4),
                    w4_raw[:, b * N * PACK : (b + 1) * N * PACK].rearrange("p (t c i) -> p c t i", t=PACK, i=4),
                )
            for lo, hi in ((0, 512), (512, 2 * N)):
                nc.vector.quantize_mx(
                    out=w4_codes[:, lo:hi].bitcast(FP8X4), scales=w4_scales[:, lo:hi], in_=woven[:, PACK * lo : PACK * hi])

        y = [psum_out.tile([P, J], F32, name="y%d" % c) for c in range(N // P)]
        shelf = keep.tile([P, (SLICES + 1) * J], F32, name="shelf")

        def a_stage(s):
            b, t = divmod(s, PACK)
            if t == 0:
                quantize_w1(b)
            if s == 0:
                v1.append(gather("v1_1", tab1[1], idx1, U32, pieces=2))
                for pair in range(2):
                    squares = ring.tile([P, 2, J], F32, name="squares", tag="early", align_bytes=64)
                    for i in range(2):
                        late = PACK + 2 * pair + i
                        nc.gpsimd.tensor_tensor(squares[:, i, :], half_sin[late], half_sin[late], ALU.mult)
                        half_sin[late] = squares[:, i, :]
            ms = slice(s * P, (s + 1) * P)
            a_win = wins.tile([P, S], F32, name="a_win", tag="win")
            first_stage(
                a_win,
                [(w1_codes[:, a, ms].bitcast(FP8X4), w1_scales[:, a, ms], v1[a], v1_scales[:, a * S : (a + 1) * S])
                 for a in range(2)],
                ACT.Identity, 0.5, a_bias[:, b, t : t + 1],
            )
            nc.vector.tensor_tensor(shelf[:, s * J : (s + 1) * J], a_win[:].indirect(p1[:]), half_sin[s], ALU.subtract)

        waves = []

        def wave_stage(s):
            b, t = divmod(s, PACK)
            u = ring.tile([P, J], F32, name="u")
            nc.scalar.activation(u[:], shelf[:, s * J : (s + 1) * J], ACT.Sin)
            wave = ring.tile([P, J], F32, name="wave", bufs=3)
            nc.vector.scalar_tensor_tensor(wave[:], u[:], neg2_zg[:, b, t : t + 1], u[:], ALU.mult, ALU.mult)
            waves.append(wave)

        def z_stage(s):
            nc.vector.tensor_tensor(shelf[:, (s + 1) * J : (s + 2) * J], d_wins[s][:].indirect(p3[:]), waves[s][:], ALU.add)
            if s % PACK < PACK - 1:
                return
            b = s // PACK
            if b == 0:
                quantize_w4()
            z32 = shelf[:, (PACK * b + 1) * J : (PACK * b + PACK + 1) * J]
            z16 = ring.tile([P, PACK * J], BF16, name="z16", tag="woven", align_bytes=64)
            nc.scalar.copy(
                z16[:].rearrange("p (c i t) -> p c t i", t=PACK, i=4),
                z32.rearrange("p (t c i) -> p c t i", t=PACK, i=4),
            )
            z_codes = ring.tile([P, J], U32, name="z_codes", align_bytes=64)
            z_scales = ring.tile([P, J], U8, name="z_scales", align_bytes=64)
            nc.vector.quantize_mx(out=z_codes[:].bitcast(FP8X4), scales=z_scales[:], in_=z16[:])
            for c in range(N // P):
                ns = slice(b * N + c * P, b * N + (c + 1) * P)
                nc.tensor.matmul_mx(
                    out=y[c][:], lhsT=w4_codes[:, ns].bitcast(FP8X4), lhsT_scale=w4_scales[:, ns],
                    rhs=z_codes[:].bitcast(FP8X4), rhs_scale=z_scales[:], start=(b == 0), stop=(b == 1),
                )

        for step in range(SLICES + 2):
            if step < SLICES:
                a_stage(step)
            if 1 <= step <= SLICES:
                wave_stage(step - 1)
            if step >= 2:
                z_stage(step - 2)

        for c in range(N // P):
            res = wins.tile([P, J], F32, name="res", tag="win")
            if c == 1:
                nc.vector.tensor_scalar(res[:], y[c][:], cols[:, 0, 8 + c : 9 + c], None, ALU.mult)
            else:
                nc.scalar.activation(res[:], y[c][:], ACT.Identity, scale=cols[:, 0, 8 + c : 9 + c])
            nc.sync.dma_start(out[c * P : (c + 1) * P, :], res[:])
